import numpy as np
import ml_dtypes


def mxq(x, axis, fmt="e4m3"):
    dtype, down = {"e4m3": (ml_dtypes.float8_e4m3fn, 7), "e5m2": (ml_dtypes.float8_e5m2, 14)}[fmt]
    v = np.moveaxis(np.asarray(x, np.float32).astype(ml_dtypes.bfloat16).astype(np.float64), axis, -1)
    blocks = v.reshape(v.shape[:-1] + (-1, 32))
    amax = np.abs(blocks).max(-1, keepdims=True)
    byte = np.maximum(np.where(amax > 0, np.frexp(amax)[1] - 1 + 127, 0) - down, 1)
    scale = np.exp2(byte - 127.0)
    codes = (blocks / scale).astype(np.float32).astype(dtype).astype(np.float64)
    return np.moveaxis((codes * scale).reshape(v.shape), -1, axis)


WIDE = False


def mx_kscale(k):
    if not WIDE:
        return np.ones(k)
    levels = np.array([30, -30])
    if k % 512:
        return np.exp2(np.random.permutation(np.resize(levels, k // 32))).repeat(32)
    a = np.empty((k // 512, 16))
    for p in range(k // 512):
        a[p, :8] = np.random.permutation(np.resize(levels, 8))
        for g in range(8):
            far = levels[np.abs(levels - a[p, g]) >= 10]
            a[p, g + 8] = far[np.random.randint(len(far))]
    return np.exp2(a.ravel()).repeat(32)


def f64(x):
    return np.asarray(x).astype(np.float64)


def striped(idx):
    return np.tile(np.asarray(idx).reshape(-1, 16).T, (8, 1)).astype(np.uint16)


def unstriped(offs):
    return offs[:16].T.reshape(-1).astype(np.int64)


E2M1 = np.array([0.0, 0.5, 1.0, 1.5, 2.0, 3.0, 4.0, 6.0, -0.0, -0.5, -1.0, -1.5, -2.0, -3.0, -4.0, -6.0])


def pack_weight(w, fmt):
    k, n = w.shape
    w = f64(np.asarray(w, np.float32).astype(ml_dtypes.bfloat16)).reshape(k // 32, 32, n)
    amax = np.abs(w).max(1)
    if fmt in ("e4m3", "e5m2"):
        byte = np.frexp(amax)[1] - 1 + 127 - (7 if fmt == "e4m3" else 14)
    else:
        mant, ex = np.frexp(amax / 6.0)
        byte = np.where(mant > 0.5, ex, ex - 1) + 127
    byte = np.clip(np.where(amax > 0, byte, 1), 1, 254)
    scaled = (w * np.exp2(127.0 - byte)[:, None, :]).reshape(k, n).astype(np.float32)
    by_word = np.ascontiguousarray(scaled.reshape(k // 512, 128, 4, n).transpose(0, 1, 3, 2))
    if fmt in ("e4m3", "e5m2"):
        words = by_word.astype(ml_dtypes.float8_e4m3fn if fmt == "e4m3" else ml_dtypes.float8_e5m2).view(np.uint8)
    else:
        c = by_word.astype(ml_dtypes.float4_e2m1fn).view(np.uint8) & 0xF
        words = (c[..., 0::2] | (c[..., 1::2] << 4)).reshape(k // 512, 128, 2 * n)
    return np.ascontiguousarray(words), np.ascontiguousarray(byte.astype(np.uint8).reshape(k // 512, 16, n))


def unpack_weight(words, scales, fmt):
    g, _, n = scales.shape
    words = np.ascontiguousarray(words).reshape(g, 128, n, -1)
    if fmt in ("e4m3", "e5m2"):
        vals = words.view(ml_dtypes.float8_e4m3fn if fmt == "e4m3" else ml_dtypes.float8_e5m2).astype(np.float64)
    else:
        nib = np.empty((g, 128, n, 4), np.uint8)
        nib[..., 0::2] = words & 0xF
        nib[..., 1::2] = words >> 4
        vals = E2M1[nib]
    vals = vals * np.repeat(np.exp2(scales.astype(np.float64) - 127.0), 8, axis=1)[..., None]
    return vals.transpose(0, 1, 3, 2).reshape(g * 512, n)


def sigmoid(v):
    return 1.0 / (1.0 + np.exp(-v))


def sgn(shape):
    return np.random.uniform(0.5, 2.0, shape) * np.where(np.random.standard_normal(shape) < 0, -1.0, 1.0)


K, T, J, R, O, N, E = 512, 1024, 256, 512, 128, 256, 512


def setup_inputs():
    n = np.random.standard_normal
    idx = np.random.permutation(T)[:J]
    idx2 = np.random.permutation(J)[:O]
    idx3 = np.random.permutation(J)[:O]
    idx4 = np.random.permutation(J)[:O]
    idx5 = np.random.permutation(J)[:O]
    idx6 = np.random.permutation(E)[:O]
    idx7 = np.random.permutation(E)[:O]
    fk = mx_kscale(K)
    fr = mx_kscale(R)
    xtp = pack_weight(n((K, T)) / fk[:, None], "e5m2")
    wp = pack_weight(n((K, R)) * 1 / np.sqrt(K) * fk[:, None], "e2m1")
    w2p = pack_weight(n((K, R)) * 1 / np.sqrt(K) * fk[:, None], "e4m3")
    wbp = pack_weight(n((R, N)) * 1 / np.sqrt(R) / fr[:, None], "e2m1")
    return {
        "xt_words": xtp[0],
        "xt_scales": xtp[1],
        "w_words": wp[0],
        "w_scales": wp[1],
        "w2_words": w2p[0],
        "w2_scales": w2p[1],
        "sa": (sgn((R, 1)) * fr[:, None]).astype(np.float32),
        "sb": (sgn((R, 1)) * fr[:, None]).astype(np.float32),
        "sg": (sgn((R, 1))).astype(np.float32),
        "bg": (np.random.uniform(-2.0, 2.0, (R, 1))).astype(np.float32),
        "sh": (sgn((R, 1))).astype(np.float32),
        "bh": (np.random.uniform(-2.0, 2.0, (R, 1))).astype(np.float32),
        "wb_words": wbp[0],
        "wb_scales": wbp[1],
        "offs": striped(idx),
        "offs2": striped(idx2),
        "offs3": striped(idx3),
        "offs4": striped(idx4),
        "offs5": striped(idx5),
        "offs6": striped(idx6),
        "offs7": striped(idx7),
    }


def reference(xt_words, xt_scales, w_words, w_scales, w2_words, w2_scales, sa, sb, sg, bg, sh, bh, wb_words, wb_scales, offs, offs2, offs3, offs4, offs5, offs6, offs7):
    idx = unstriped(offs)
    idx2 = unstriped(offs2)
    idx3 = unstriped(offs3)
    idx4 = unstriped(offs4)
    idx5 = unstriped(offs5)
    idx6 = unstriped(offs6)
    idx7 = unstriped(offs7)
    xtu = unpack_weight(xt_words, xt_scales, "e5m2")
    wu = unpack_weight(w_words, w_scales, "e2m1")
    w2u = unpack_weight(w2_words, w2_scales, "e4m3")
    wbu = unpack_weight(wb_words, wb_scales, "e2m1")
    xtidxg = xtu[:, idx]
    a = wu.T @ xtidxg
    b = w2u.T @ xtidxg
    hid = np.maximum(a[:, idx2] * f64(sa) * sigmoid(a[:, idx3] * f64(sg) + f64(bg)) + b[:, idx4] * f64(sb) * sigmoid(b[:, idx5] * f64(sh) + f64(bh)), 0.0)
    hidq = mxq(hid, 0, "e4m3")
    p = wbu.T @ hidq
    pa = np.zeros((N, E))
    pa[:, idx6] = p
    pb = np.zeros((N, E))
    pb[:, idx7] = p
    y = pa + pb
    return y

@@ -1,0 +1,192 @@
+from contextlib import ExitStack
+
+import concourse.mybir as mybir
+
+K, T, J, R, O, N, E = 512, 1024, 256, 512, 128, 256, 512
+FLOPS = 2 * (2 * K * R * J + R * N * O)
+
+F32 = mybir.dt.float32
+BF16 = mybir.dt.bfloat16
+I32 = mybir.dt.int32
+U32 = mybir.dt.uint32
+U16 = mybir.dt.uint16
+U8 = mybir.dt.uint8
+E4M3X4 = mybir.dt.float8_e4m3fn_x4
+E5M2X4 = mybir.dt.float8_e5m2_x4
+E2M1X4 = mybir.dt.float4_e2m1fn_x4
+ACT = mybir.ActivationFunctionType
+ALU = mybir.AluOpType
+
+P = 128
+PACK = 4
+QUADS = 4
+QUAD = 32
+
+
+def tile_list_gatedsum_twow_one_pagetwice_kernel(
+    tc, xt_words, xt_scales, w_words, w_scales, w2_words, w2_scales, sa, sb, sg, bg, sh, bh,
+    wb_words, wb_scales, offs, offs2, offs3, offs4, offs5, offs6, offs7, out,
+):
+    nc = tc.nc
+    with ExitStack() as ctx:
+        lists = ctx.enter_context(tc.tile_pool(name="lists", bufs=1))
+        keep = ctx.enter_context(tc.tile_pool(name="keep", bufs=1))
+        psum = ctx.enter_context(tc.psum_pool(name="psum", bufs=1))
+
+        def load_list(src, name):
+            tile = lists.tile(list(src.shape), U16, name=name)
+            nc.sync.dma_start(tile[:], src)
+            return tile
+
+        def load_rows(src, name):
+            tile = keep.tile([P, PACK], F32, name=name)
+            nc.sync.dma_start(tile[:], src.rearrange("(p t) one -> p (t one)", t=PACK))
+            return tile
+
+        def load_scale_rows(src, name):
+            words = src.shape[2] // 4
+            tile = keep.tile([4, QUADS, words], I32, name=name)
+            nc.sync.dma_start(tile[:], src[0].bitcast(I32).rearrange("(q r) c -> r q c", q=QUADS))
+            return tile
+
+        def zeroed_plane(width, name):
+            plane = keep.tile([P, width], U8, name=name, align_bytes=64)
+            nc.vector.memset(plane[:].bitcast(I32), 0)
+            return plane
+
+        def spread(plane, staged):
+            for q in range(QUADS):
+                nc.vector.tensor_copy(plane[QUAD * q : QUAD * q + 4, :].bitcast(I32), staged[:, q, :])
+
+        def deal(dst, src, copy=nc.vector.tensor_copy):
+            copy(
+                dst.rearrange("p (t m) -> p m t", t=PACK), src.rearrange("p (m t) -> p m t", t=PACK)
+            )
+
+        def load_plane(plane, src):
+            for q in range(QUADS):
+                nc.sync.dma_start(plane[QUAD * q : QUAD * q + 4, :].bitcast(I32), src[0, 4 * q : 4 * q + 4, :].bitcast(I32))
+
+        x_plane = zeroed_plane(T, "x_plane")
+        w_plane = zeroed_plane(R, "w_plane")
+        w2_plane = zeroed_plane(R, "w2_plane")
+        wb_plane = zeroed_plane(N, "wb_plane")
+        pages = {}
+        for h in range(2):
+            for name, engine in (("pa", nc.vector), ("pb", nc.gpsimd)):
+                page = keep.tile([P, E], F32, name=f"{name}{h}")
+                engine.memset(page[:], 0.0)
+                pages[name, h] = page
+
+        x_rows = load_scale_rows(xt_scales, "x_rows")
+        w_raw = keep.tile([P, 2 * R], U8, name="w_raw", align_bytes=64)
+        nc.scalar.dma_start(w_raw[:].bitcast(I32), w_words[0].bitcast(I32))
+        w_rows = load_scale_rows(w_scales, "w_rows")
+        x_words = keep.tile([P, T], U32, name="x_words", align_bytes=64)
+        nc.scalar.dma_start(x_words[:].bitcast(I32), xt_words[0].rearrange("p c t -> p (c t)").bitcast(I32))
+        slot_list = load_list(offs, "slot_list")
+        list3 = load_list(offs3, "list3")
+        sg_t = load_rows(sg, "sg_t")
+        bg_t = load_rows(bg, "bg_t")
+        list2 = load_list(offs2, "list2")
+        sa_t = load_rows(sa, "sa_t")
+        load_plane(w2_plane, w2_scales)
+        w2_raw = keep.tile([P, R], U32, name="w2_raw", align_bytes=64)
+        nc.sync.dma_start(w2_raw[:].bitcast(I32), w2_words[0].rearrange("p c t -> p (c t)").bitcast(I32))
+        list5 = load_list(offs5, "list5")
+        sh_t = load_rows(sh, "sh_t")
+        bh_t = load_rows(bh, "bh_t")
+        list4 = load_list(offs4, "list4")
+        sb_t = load_rows(sb, "sb_t")
+        load_plane(wb_plane, wb_scales)
+        wb_codes = keep.tile([P, 2 * N], U8, name="wb_codes", align_bytes=64)
+        nc.sync.dma_start(wb_codes[:].bitcast(I32), wb_words[0].bitcast(I32))
+        list6 = load_list(offs6, "list6")
+        list7 = load_list(offs7, "list7")
+
+        spread(x_plane, x_rows)
+        spread(w_plane, w_rows)
+        xg_scales = keep.tile([P, J], U8, name="xg_scales", align_bytes=64)
+        nc.vector.tensor_copy(xg_scales[:], x_plane[:].indirect(slot_list[:]))
+        w_dealt_plane = keep.tile([P, R], U8, name="w_dealt_plane", align_bytes=64)
+        deal(w_dealt_plane[:], w_plane[:])
+        w_codes = keep.tile([P, 2 * R], U8, name="w_codes", align_bytes=64)
+        deal(w_codes[:].bitcast(U16), w_raw[:].bitcast(U16), nc.scalar.copy)
+        xg_words = keep.tile([P, J], U32, name="xg_words", align_bytes=64)
+        nc.vector.tensor_copy(xg_words[:], x_words[:].indirect(slot_list[:]))
+
+        def first_stage(name, lhs_of, plane):
+            tiles = []
+            for t in range(PACK):
+                acc = psum.tile([P, J], F32, name=f"acc_{name}{t}", tag=f"bank_{name}{t}")
+                nc.tensor.matmul_mx(
+                    acc[:], lhsT=lhs_of(t), lhsT_scale=plane[:, P * t : P * (t + 1)],
+                    rhs=xg_words[:].bitcast(E5M2X4), rhs_scale=xg_scales[:], start=True, stop=True,
+                )
+                rows = keep.tile([P, J], F32, name=f"{name}{t}")
+                nc.vector.tensor_copy(rows[:], acc[:])
+                tiles.append(rows)
+            return tiles
+
+        def looks(tiles, val, gate, val_list, gate_list, weight, slope, offset):
+            for t in range(PACK):
+                col = slice(t, t + 1)
+                nc.scalar.activation(
+                    gate[:, t, :], tiles[t][:].indirect(gate_list[:]), ACT.Sigmoid,
+                    bias=offset[:, col], scale=slope[:, col],
+                )
+                nc.scalar.activation(val[:, t, :], tiles[t][:].indirect(val_list[:]), ACT.Copy, scale=weight[:, col])
+
+        a_tiles = first_stage("a", lambda t: w_codes[:, 2 * P * t : 2 * P * (t + 1)].bitcast(E2M1X4), w_dealt_plane)
+        a_val = keep.tile([P, PACK, O], F32, name="a_val")
+        a_gate = keep.tile([P, PACK, O], F32, name="a_gate")
+        looks(a_tiles, a_val, a_gate, list2, list3, sa_t, sg_t, bg_t)
+
+        w2_dealt_plane = keep.tile([P, R], U8, name="w2_dealt_plane", align_bytes=64)
+        deal(w2_dealt_plane[:], w2_plane[:])
+        w2_codes = keep.tile([P, R], U32, name="w2_codes", align_bytes=64)
+        deal(w2_codes[:], w2_raw[:])
+        b_tiles = first_stage("b", lambda t: w2_codes[:, P * t : P * (t + 1)].bitcast(E4M3X4), w2_dealt_plane)
+        b_val = keep.tile([P, PACK, O], F32, name="b_val")
+        b_gate = keep.tile([P, PACK, O], F32, name="b_gate")
+        looks(b_tiles, b_val, b_gate, list4, list5, sb_t, sh_t, bh_t)
+
+        a_term = keep.tile([P, PACK, O], F32, name="a_term")
+        b_term = keep.tile([P, PACK, O], F32, name="b_term")
+        summed = keep.tile([P, PACK, O], F32, name="summed")
+        nc.vector.tensor_tensor(a_term[:], a_val[:], a_gate[:], ALU.mult)
+        hid = keep.tile([P, O, PACK], BF16, name="hid", align_bytes=64)
+        for lo, hi in ((0, 2), (2, 3), (3, 4)):
+            nc.vector.tensor_tensor(b_term[:, lo:hi, :], b_val[:, lo:hi, :], b_gate[:, lo:hi, :], ALU.mult)
+            nc.vector.tensor_tensor(summed[:, lo:hi, :], a_term[:, lo:hi, :], b_term[:, lo:hi, :], ALU.add)
+            if hi % 2 == 0:
+                nc.vector.tensor_scalar_max(
+                    hid[:, :, hi - 2 : hi], summed[:, hi - 2 : hi, :].rearrange("p t o -> p o t"), 0.0
+                )
+        hid_codes = keep.tile([P, O], U32, name="hid_codes", align_bytes=64)
+        hid_scales = keep.tile([P, O], U8, name="hid_scales", align_bytes=64)
+        nc.vector.quantize_mx(hid_codes[:].bitcast(E4M3X4), hid_scales[:], hid[:].rearrange("p o t -> p (o t)"))
+
+        p_tiles = []
+        for h in range(2):
+            acc = psum.tile([P, O], F32, name=f"acc_p{h}", tag=f"bank_a{h}")
+            nc.tensor.matmul_mx(
+                acc[:], lhsT=wb_codes[:, 2 * P * h : 2 * P * (h + 1)].bitcast(E2M1X4),
+                lhsT_scale=wb_plane[:, P * h : P * (h + 1)],
+                rhs=hid_codes[:].bitcast(E4M3X4), rhs_scale=hid_scales[:], start=True, stop=True,
+            )
+            rows = keep.tile([P, O], F32, name=f"p{h}")
+            if h == 0:
+                nc.vector.tensor_copy(rows[:], acc[:])
+            else:
+                nc.scalar.copy(rows[:], acc[:])
+            p_tiles.append(rows)
+        for h in range(2):
+            nc.vector.tensor_copy(pages["pa", h][:].indirect(list6[:]), p_tiles[h][:])
+            nc.scalar.activation(pages["pb", h][:].indirect(list7[:]), p_tiles[h][:], ACT.Copy)
+            pieces = h + 1
+            for piece in range(pieces):
+                cols = slice(E // pieces * piece, E // pieces * (piece + 1))
+                total = keep.tile([P, E // pieces], F32, name=f"total{h}{piece}")
+                nc.vector.tensor_tensor(total[:], pages["pa", h][:, cols], pages["pb", h][:, cols], ALU.add)
+                nc.sync.dma_start(out[P * h : P * (h + 1), cols], total[:])

@@ -38,15 +38,15 @@ def tile_list_gatedsum_twow_one_pagetwice_kernel(
             nc.sync.dma_start(tile[:], src)
             return tile
 
-        def load_rows(src, name):
+        def load_rows(src, name, queue=nc.sync):
             tile = keep.tile([P, PACK], F32, name=name)
-            nc.sync.dma_start(tile[:], src.rearrange("(p t) one -> p (t one)", t=PACK))
+            queue.dma_start(tile[:], src.rearrange("(p t) one -> p (t one)", t=PACK))
             return tile
 
-        def load_scale_rows(src, name):
+        def load_scale_rows(src, name, queue=nc.sync):
             words = src.shape[2] // 4
             tile = keep.tile([4, QUADS, words], I32, name=name)
-            nc.sync.dma_start(tile[:], src[0].bitcast(I32).rearrange("(q r) c -> r q c", q=QUADS))
+            queue.dma_start(tile[:], src[0].bitcast(I32).rearrange("(q r) c -> r q c", q=QUADS))
             return tile
 
         def zeroed_plane(width, name):
@@ -58,14 +58,11 @@ def tile_list_gatedsum_twow_one_pagetwice_kernel(
             for q in range(QUADS):
                 nc.vector.tensor_copy(plane[QUAD * q : QUAD * q + 4, :].bitcast(I32), staged[:, q, :])
 
-        def deal(dst, src, copy=nc.vector.tensor_copy):
-            copy(
-                dst.rearrange("p (t m) -> p m t", t=PACK), src.rearrange("p (m t) -> p m t", t=PACK)
+        def deal(dst, src, lo, hi):
+            nc.vector.tensor_copy(
+                dst.rearrange("p (t m) -> p m t", t=PACK)[:, :, lo:hi],
+                src.rearrange("p (m t) -> p m t", t=PACK)[:, :, lo:hi],
             )
-
-        def load_plane(plane, src):
-            for q in range(QUADS):
-                nc.sync.dma_start(plane[QUAD * q : QUAD * q + 4, :].bitcast(I32), src[0, 4 * q : 4 * q + 4, :].bitcast(I32))
 
         x_plane = zeroed_plane(T, "x_plane")
         w_plane = zeroed_plane(R, "w_plane")
@@ -78,19 +75,19 @@ def tile_list_gatedsum_twow_one_pagetwice_kernel(
                 engine.memset(page[:], 0.0)
                 pages[name, h] = page
 
+        slot_list = load_list(offs, "slot_list")
+        sg_t = load_rows(sg, "sg_t", nc.scalar)
         x_rows = load_scale_rows(xt_scales, "x_rows")
-        w_raw = keep.tile([P, 2 * R], U8, name="w_raw", align_bytes=64)
-        nc.scalar.dma_start(w_raw[:].bitcast(I32), w_words[0].bitcast(I32))
-        w_rows = load_scale_rows(w_scales, "w_rows")
+        bg_t = load_rows(bg, "bg_t", nc.scalar)
+        list3 = load_list(offs3, "list3")
+        w_rows = load_scale_rows(w_scales, "w_rows", nc.scalar)
         x_words = keep.tile([P, T], U32, name="x_words", align_bytes=64)
         nc.scalar.dma_start(x_words[:].bitcast(I32), xt_words[0].rearrange("p c t -> p (c t)").bitcast(I32))
-        slot_list = load_list(offs, "slot_list")
-        list3 = load_list(offs3, "list3")
-        sg_t = load_rows(sg, "sg_t")
-        bg_t = load_rows(bg, "bg_t")
+        w_raw = keep.tile([P, 2 * R], U8, name="w_raw", align_bytes=64)
+        nc.scalar.dma_start(w_raw[:].bitcast(I32), w_words[0].bitcast(I32))
+        w2_rows = load_scale_rows(w2_scales, "w2_rows")
         list2 = load_list(offs2, "list2")
         sa_t = load_rows(sa, "sa_t")
-        load_plane(w2_plane, w2_scales)
         w2_raw = keep.tile([P, R], U32, name="w2_raw", align_bytes=64)
         nc.sync.dma_start(w2_raw[:].bitcast(I32), w2_words[0].rearrange("p c t -> p (c t)").bitcast(I32))
         list5 = load_list(offs5, "list5")
@@ -98,7 +95,7 @@ def tile_list_gatedsum_twow_one_pagetwice_kernel(
         bh_t = load_rows(bh, "bh_t")
         list4 = load_list(offs4, "list4")
         sb_t = load_rows(sb, "sb_t")
-        load_plane(wb_plane, wb_scales)
+        wb_rows = load_scale_rows(wb_scales, "wb_rows")
         wb_codes = keep.tile([P, 2 * N], U8, name="wb_codes", align_bytes=64)
         nc.sync.dma_start(wb_codes[:].bitcast(I32), wb_words[0].bitcast(I32))
         list6 = load_list(offs6, "list6")
@@ -109,49 +106,54 @@ def tile_list_gatedsum_twow_one_pagetwice_kernel(
         xg_scales = keep.tile([P, J], U8, name="xg_scales", align_bytes=64)
         nc.vector.tensor_copy(xg_scales[:], x_plane[:].indirect(slot_list[:]))
         w_dealt_plane = keep.tile([P, R], U8, name="w_dealt_plane", align_bytes=64)
-        deal(w_dealt_plane[:], w_plane[:])
         w_codes = keep.tile([P, 2 * R], U8, name="w_codes", align_bytes=64)
-        deal(w_codes[:].bitcast(U16), w_raw[:].bitcast(U16), nc.scalar.copy)
+        deal(w_dealt_plane[:], w_plane[:], 0, 1)
         xg_words = keep.tile([P, J], U32, name="xg_words", align_bytes=64)
         nc.vector.tensor_copy(xg_words[:], x_words[:].indirect(slot_list[:]))
+        deal(w_codes[:].bitcast(U16), w_raw[:].bitcast(U16), 0, 1)
+        deal(w_dealt_plane[:], w_plane[:], 1, PACK)
+        deal(w_codes[:].bitcast(U16), w_raw[:].bitcast(U16), 1, PACK)
 
-        def first_stage(name, lhs_of, plane):
-            tiles = []
-            for t in range(PACK):
-                acc = psum.tile([P, J], F32, name=f"acc_{name}{t}", tag=f"bank_{name}{t}")
-                nc.tensor.matmul_mx(
-                    acc[:], lhsT=lhs_of(t), lhsT_scale=plane[:, P * t : P * (t + 1)],
-                    rhs=xg_words[:].bitcast(E5M2X4), rhs_scale=xg_scales[:], start=True, stop=True,
-                )
-                rows = keep.tile([P, J], F32, name=f"{name}{t}")
-                nc.vector.tensor_copy(rows[:], acc[:])
-                tiles.append(rows)
-            return tiles
+        def product(name, t, codes, plane):
+            acc = psum.tile([P, J], F32, name=f"acc_{name}{t}", tag=f"bank_{name}{t}")
+            nc.tensor.matmul_mx(
+                acc[:], lhsT=codes, lhsT_scale=plane[:, P * t : P * (t + 1)],
+                rhs=xg_words[:].bitcast(E5M2X4), rhs_scale=xg_scales[:], start=True, stop=True,
+            )
+            return acc
 
-        def looks(tiles, val, gate, val_list, gate_list, weight, slope, offset):
-            for t in range(PACK):
-                col = slice(t, t + 1)
-                nc.scalar.activation(
-                    gate[:, t, :], tiles[t][:].indirect(gate_list[:]), ACT.Sigmoid,
-                    bias=offset[:, col], scale=slope[:, col],
-                )
-                nc.scalar.activation(val[:, t, :], tiles[t][:].indirect(val_list[:]), ACT.Copy, scale=weight[:, col])
+        def looks(name, t, acc, val, gate, val_list, gate_list, weight, slope, offset):
+            rows = keep.tile([P, J], F32, name=f"{name}{t}")
+            nc.vector.tensor_copy(rows[:], acc[:])
+            col = slice(t, t + 1)
+            nc.scalar.activation(
+                gate[:, t, :], rows[:].indirect(gate_list[:]), ACT.Sigmoid, bias=offset[:, col], scale=slope[:, col]
+            )
+            nc.scalar.activation(val[:, t, :], rows[:].indirect(val_list[:]), ACT.Copy, scale=weight[:, col])
 
-        a_tiles = first_stage("a", lambda t: w_codes[:, 2 * P * t : 2 * P * (t + 1)].bitcast(E2M1X4), w_dealt_plane)
         a_val = keep.tile([P, PACK, O], F32, name="a_val")
         a_gate = keep.tile([P, PACK, O], F32, name="a_gate")
-        looks(a_tiles, a_val, a_gate, list2, list3, sa_t, sg_t, bg_t)
-
-        w2_dealt_plane = keep.tile([P, R], U8, name="w2_dealt_plane", align_bytes=64)
-        deal(w2_dealt_plane[:], w2_plane[:])
-        w2_codes = keep.tile([P, R], U32, name="w2_codes", align_bytes=64)
-        deal(w2_codes[:], w2_raw[:])
-        b_tiles = first_stage("b", lambda t: w2_codes[:, P * t : P * (t + 1)].bitcast(E4M3X4), w2_dealt_plane)
         b_val = keep.tile([P, PACK, O], F32, name="b_val")
         b_gate = keep.tile([P, PACK, O], F32, name="b_gate")
-        looks(b_tiles, b_val, b_gate, list4, list5, sb_t, sh_t, bh_t)
+        w2_dealt_plane = keep.tile([P, R], U8, name="w2_dealt_plane", align_bytes=64)
+        w2_codes = keep.tile([P, R], U32, name="w2_codes", tag="w2_codes", align_bytes=64)
 
-        a_term = keep.tile([P, PACK, O], F32, name="a_term")
+        a_acc = [
+            product("a", t, w_codes[:, 2 * P * t : 2 * P * (t + 1)].bitcast(E2M1X4), w_dealt_plane) for t in range(PACK)
+        ]
+        for t in range(PACK):
+            looks("a", t, a_acc[t], a_val, a_gate, list2, list3, sa_t, sg_t, bg_t)
+            if t == 1:
+                spread(w2_plane, w2_rows)
+                deal(w2_dealt_plane[:], w2_plane[:], 0, PACK)
+            if t == 2:
+                deal(w2_codes[:], w2_raw[:], 0, PACK)
+        for t in range(PACK):
+            acc = product("b", t, w2_codes[:, P * t : P * (t + 1)].bitcast(E4M3X4), w2_dealt_plane)
+            looks("b", t, acc, b_val, b_gate, list4, list5, sb_t, sh_t, bh_t)
+
+        spread(wb_plane, wb_rows)
+        a_term = keep.tile([P, PACK, O], F32, name="a_term", tag="w2_codes", align_bytes=64)
         b_term = keep.tile([P, PACK, O], F32, name="b_term")
         summed = keep.tile([P, PACK, O], F32, name="summed")
         nc.vector.tensor_tensor(a_term[:], a_val[:], a_gate[:], ALU.mult)
@@ -184,7 +186,7 @@ def tile_list_gatedsum_twow_one_pagetwice_kernel(
         for h in range(2):
             nc.vector.tensor_copy(pages["pa", h][:].indirect(list6[:]), p_tiles[h][:])
             nc.scalar.activation(pages["pb", h][:].indirect(list7[:]), p_tiles[h][:], ACT.Copy)
-            pieces = h + 1
+            pieces = 2
             for piece in range(pieces):
                 cols = slice(E // pieces * piece, E // pieces * (piece + 1))
                 total = keep.tile([P, E // pieces], F32, name=f"total{h}{piece}")

@@ -58,10 +58,14 @@ def tile_list_gatedsum_twow_one_pagetwice_kernel(
             for q in range(QUADS):
                 nc.vector.tensor_copy(plane[QUAD * q : QUAD * q + 4, :].bitcast(I32), staged[:, q, :])
 
-        def deal(dst, src, lo, hi):
+        def deal(dst, src):
             nc.vector.tensor_copy(
-                dst.rearrange("p (t m) -> p m t", t=PACK)[:, :, lo:hi],
-                src.rearrange("p (m t) -> p m t", t=PACK)[:, :, lo:hi],
+                dst.rearrange("p (t m) -> p t m", t=PACK), src.rearrange("p (m t) -> p t m", t=PACK)
+            )
+
+        def deal_words(dst, src):
+            nc.vector.tensor_copy(
+                dst.rearrange("p (t c i) -> p c t i", t=PACK, i=4), src.rearrange("p (c i t) -> p c t i", t=PACK, i=4)
             )
 
         x_plane = zeroed_plane(T, "x_plane")
@@ -75,16 +79,16 @@ def tile_list_gatedsum_twow_one_pagetwice_kernel(
                 engine.memset(page[:], 0.0)
                 pages[name, h] = page
 
-        slot_list = load_list(offs, "slot_list")
+        w_rows = load_scale_rows(w_scales, "w_rows")
         sg_t = load_rows(sg, "sg_t", nc.scalar)
         x_rows = load_scale_rows(xt_scales, "x_rows")
-        bg_t = load_rows(bg, "bg_t", nc.scalar)
-        list3 = load_list(offs3, "list3")
-        w_rows = load_scale_rows(w_scales, "w_rows", nc.scalar)
-        x_words = keep.tile([P, T], U32, name="x_words", align_bytes=64)
-        nc.scalar.dma_start(x_words[:].bitcast(I32), xt_words[0].rearrange("p c t -> p (c t)").bitcast(I32))
         w_raw = keep.tile([P, 2 * R], U8, name="w_raw", align_bytes=64)
         nc.scalar.dma_start(w_raw[:].bitcast(I32), w_words[0].bitcast(I32))
+        slot_list = load_list(offs, "slot_list")
+        x_words = keep.tile([P, T], U32, name="x_words", align_bytes=64)
+        nc.scalar.dma_start(x_words[:].bitcast(I32), xt_words[0].rearrange("p c t -> p (c t)").bitcast(I32))
+        list3 = load_list(offs3, "list3")
+        bg_t = load_rows(bg, "bg_t")
         w2_rows = load_scale_rows(w2_scales, "w2_rows")
         list2 = load_list(offs2, "list2")
         sa_t = load_rows(sa, "sa_t")
@@ -95,36 +99,52 @@ def tile_list_gatedsum_twow_one_pagetwice_kernel(
         bh_t = load_rows(bh, "bh_t")
         list4 = load_list(offs4, "list4")
         sb_t = load_rows(sb, "sb_t")
-        wb_rows = load_scale_rows(wb_scales, "wb_rows")
+        for q in range(QUADS):
+            nc.sync.dma_start(
+                wb_plane[QUAD * q : QUAD * q + 4, :].bitcast(I32), wb_scales[0, 4 * q : 4 * q + 4, :].bitcast(I32)
+            )
         wb_codes = keep.tile([P, 2 * N], U8, name="wb_codes", align_bytes=64)
         nc.sync.dma_start(wb_codes[:].bitcast(I32), wb_words[0].bitcast(I32))
         list6 = load_list(offs6, "list6")
         list7 = load_list(offs7, "list7")
 
-        spread(x_plane, x_rows)
-        spread(w_plane, w_rows)
-        xg_scales = keep.tile([P, J], U8, name="xg_scales", align_bytes=64)
-        nc.vector.tensor_copy(xg_scales[:], x_plane[:].indirect(slot_list[:]))
         w_dealt_plane = keep.tile([P, R], U8, name="w_dealt_plane", align_bytes=64)
         w_codes = keep.tile([P, 2 * R], U8, name="w_codes", align_bytes=64)
-        deal(w_dealt_plane[:], w_plane[:], 0, 1)
+        xg_scales = keep.tile([P, J], U8, name="xg_scales", align_bytes=64)
         xg_words = keep.tile([P, J], U32, name="xg_words", align_bytes=64)
-        nc.vector.tensor_copy(xg_words[:], x_words[:].indirect(slot_list[:]))
-        deal(w_codes[:].bitcast(U16), w_raw[:].bitcast(U16), 0, 1)
-        deal(w_dealt_plane[:], w_plane[:], 1, PACK)
-        deal(w_codes[:].bitcast(U16), w_raw[:].bitcast(U16), 1, PACK)
-
-        def product(name, t, codes, plane):
-            acc = psum.tile([P, J], F32, name=f"acc_{name}{t}", tag=f"bank_{name}{t}")
-            nc.tensor.matmul_mx(
-                acc[:], lhsT=codes, lhsT_scale=plane[:, P * t : P * (t + 1)],
-                rhs=xg_words[:].bitcast(E5M2X4), rhs_scale=xg_scales[:], start=True, stop=True,
+        spread(w_plane, w_rows)
+        deal(w_dealt_plane[:], w_plane[:])
+        spread(x_plane, x_rows)
+        deal(w_codes[:].bitcast(U16), w_raw[:].bitcast(U16))
+        nc.vector.tensor_copy(xg_scales[:], x_plane[:].indirect(slot_list[:]))
+        for half in range(2):
+            nc.vector.tensor_copy(
+                xg_words[:, J // 2 * half : J // 2 * (half + 1)],
+                x_words[:].indirect(slot_list[:, J // 32 * half : J // 32 * (half + 1)]),
             )
-            return acc
 
-        def looks(name, t, acc, val, gate, val_list, gate_list, weight, slope, offset):
+        spread(w2_plane, w2_rows)
+
+        banks = list(range(8))
+
+        def product(name, t, codes, plane, pieces=1):
+            accs = []
+            for piece in range(pieces):
+                cols = slice(J // pieces * piece, J // pieces * (piece + 1))
+                bank = banks.pop(0)
+                banks.append(bank)
+                acc = psum.tile([P, J // pieces], F32, name=f"acc_{name}{t}_{piece}", tag=f"bank{bank}")
+                nc.tensor.matmul_mx(
+                    acc[:], lhsT=codes, lhsT_scale=plane[:, P * t : P * (t + 1)],
+                    rhs=xg_words[:, cols].bitcast(E5M2X4), rhs_scale=xg_scales[:, cols], start=True, stop=True,
+                )
+                accs.append((cols, acc))
+            return accs
+
+        def looks(name, t, accs, val, gate, val_list, gate_list, weight, slope, offset):
             rows = keep.tile([P, J], F32, name=f"{name}{t}")
-            nc.vector.tensor_copy(rows[:], acc[:])
+            for cols, acc in accs:
+                nc.vector.tensor_copy(rows[:, cols], acc[:])
             col = slice(t, t + 1)
             nc.scalar.activation(
                 gate[:, t, :], rows[:].indirect(gate_list[:]), ACT.Sigmoid, bias=offset[:, col], scale=slope[:, col]
@@ -139,20 +159,19 @@ def tile_list_gatedsum_twow_one_pagetwice_kernel(
         w2_codes = keep.tile([P, R], U32, name="w2_codes", tag="w2_codes", align_bytes=64)
 
         a_acc = [
-            product("a", t, w_codes[:, 2 * P * t : 2 * P * (t + 1)].bitcast(E2M1X4), w_dealt_plane) for t in range(PACK)
+            product("a", t, w_codes[:, 2 * P * t : 2 * P * (t + 1)].bitcast(E2M1X4), w_dealt_plane, 2 if t == 0 else 1)
+            for t in range(PACK)
         ]
         for t in range(PACK):
             looks("a", t, a_acc[t], a_val, a_gate, list2, list3, sa_t, sg_t, bg_t)
+            if t == 0:
+                deal(w2_dealt_plane[:], w2_plane[:])
             if t == 1:
-                spread(w2_plane, w2_rows)
-                deal(w2_dealt_plane[:], w2_plane[:], 0, PACK)
-            if t == 2:
-                deal(w2_codes[:], w2_raw[:], 0, PACK)
+                deal_words(w2_codes[:], w2_raw[:])
         for t in range(PACK):
             acc = product("b", t, w2_codes[:, P * t : P * (t + 1)].bitcast(E4M3X4), w2_dealt_plane)
             looks("b", t, acc, b_val, b_gate, list4, list5, sb_t, sh_t, bh_t)
 
-        spread(wb_plane, wb_rows)
         a_term = keep.tile([P, PACK, O], F32, name="a_term", tag="w2_codes", align_bytes=64)
         b_term = keep.tile([P, PACK, O], F32, name="b_term")
         summed = keep.tile([P, PACK, O], F32, name="summed")
@@ -161,17 +180,14 @@ def tile_list_gatedsum_twow_one_pagetwice_kernel(
         for lo, hi in ((0, 2), (2, 3), (3, 4)):
             nc.vector.tensor_tensor(b_term[:, lo:hi, :], b_val[:, lo:hi, :], b_gate[:, lo:hi, :], ALU.mult)
             nc.vector.tensor_tensor(summed[:, lo:hi, :], a_term[:, lo:hi, :], b_term[:, lo:hi, :], ALU.add)
-            if hi % 2 == 0:
-                nc.vector.tensor_scalar_max(
-                    hid[:, :, hi - 2 : hi], summed[:, hi - 2 : hi, :].rearrange("p t o -> p o t"), 0.0
-                )
+        nc.vector.tensor_scalar_max(hid[:], summed[:].rearrange("p t o -> p o t"), 0.0)
         hid_codes = keep.tile([P, O], U32, name="hid_codes", align_bytes=64)
         hid_scales = keep.tile([P, O], U8, name="hid_scales", align_bytes=64)
         nc.vector.quantize_mx(hid_codes[:].bitcast(E4M3X4), hid_scales[:], hid[:].rearrange("p o t -> p (o t)"))
 
         p_tiles = []
         for h in range(2):
-            acc = psum.tile([P, O], F32, name=f"acc_p{h}", tag=f"bank_a{h}")
+            acc = psum.tile([P, O], F32, name=f"acc_p{h}", tag=f"bank{1 + h}")
             nc.tensor.matmul_mx(
                 acc[:], lhsT=wb_codes[:, 2 * P * h : 2 * P * (h + 1)].bitcast(E2M1X4),
                 lhsT_scale=wb_plane[:, P * h : P * (h + 1)],

@@ -54,13 +54,19 @@ def tile_list_gatedsum_twow_one_pagetwice_kernel(
             nc.vector.memset(plane[:].bitcast(I32), 0)
             return plane
 
+        def load_plane(plane, src):
+            for q in range(QUADS):
+                nc.sync.dma_start(
+                    plane[QUAD * q : QUAD * q + 4, :].bitcast(I32), src[0, 4 * q : 4 * q + 4, :].bitcast(I32)
+                )
+
         def spread(plane, staged):
             for q in range(QUADS):
                 nc.vector.tensor_copy(plane[QUAD * q : QUAD * q + 4, :].bitcast(I32), staged[:, q, :])
 
-        def deal(dst, src):
+        def deal(dst, src, lo=0, hi=PACK):
             nc.vector.tensor_copy(
-                dst.rearrange("p (t m) -> p t m", t=PACK), src.rearrange("p (m t) -> p t m", t=PACK)
+                dst.rearrange("p (t m) -> p t m", m=P), src.rearrange("p (m t) -> p t m", t=PACK)[:, lo:hi, :]
             )
 
         def deal_words(dst, src):
@@ -72,12 +78,6 @@ def tile_list_gatedsum_twow_one_pagetwice_kernel(
         w_plane = zeroed_plane(R, "w_plane")
         w2_plane = zeroed_plane(R, "w2_plane")
         wb_plane = zeroed_plane(N, "wb_plane")
-        pages = {}
-        for h in range(2):
-            for name, engine in (("pa", nc.vector), ("pb", nc.gpsimd)):
-                page = keep.tile([P, E], F32, name=f"{name}{h}")
-                engine.memset(page[:], 0.0)
-                pages[name, h] = page
 
         w_rows = load_scale_rows(w_scales, "w_rows")
         sg_t = load_rows(sg, "sg_t", nc.scalar)
@@ -85,45 +85,45 @@ def tile_list_gatedsum_twow_one_pagetwice_kernel(
         w_raw = keep.tile([P, 2 * R], U8, name="w_raw", align_bytes=64)
         nc.scalar.dma_start(w_raw[:].bitcast(I32), w_words[0].bitcast(I32))
         slot_list = load_list(offs, "slot_list")
-        x_words = keep.tile([P, T], U32, name="x_words", align_bytes=64)
+        x_words = keep.tile([P, T], U32, name="x_words", tag="x_words", align_bytes=64)
         nc.scalar.dma_start(x_words[:].bitcast(I32), xt_words[0].rearrange("p c t -> p (c t)").bitcast(I32))
         list3 = load_list(offs3, "list3")
         bg_t = load_rows(bg, "bg_t")
-        w2_rows = load_scale_rows(w2_scales, "w2_rows")
+        sh_t = load_rows(sh, "sh_t", nc.gpsimd)
+        bh_t = load_rows(bh, "bh_t", nc.gpsimd)
         list2 = load_list(offs2, "list2")
         sa_t = load_rows(sa, "sa_t")
-        w2_raw = keep.tile([P, R], U32, name="w2_raw", align_bytes=64)
-        nc.sync.dma_start(w2_raw[:].bitcast(I32), w2_words[0].rearrange("p c t -> p (c t)").bitcast(I32))
         list5 = load_list(offs5, "list5")
-        sh_t = load_rows(sh, "sh_t")
-        bh_t = load_rows(bh, "bh_t")
         list4 = load_list(offs4, "list4")
         sb_t = load_rows(sb, "sb_t")
-        for q in range(QUADS):
-            nc.sync.dma_start(
-                wb_plane[QUAD * q : QUAD * q + 4, :].bitcast(I32), wb_scales[0, 4 * q : 4 * q + 4, :].bitcast(I32)
-            )
+        load_plane(w2_plane, w2_scales)
+        w2_raw = keep.tile([P, R], U32, name="w2_raw", align_bytes=64)
+        nc.sync.dma_start(w2_raw[:].bitcast(I32), w2_words[0].rearrange("p c t -> p (c t)").bitcast(I32))
+        load_plane(wb_plane, wb_scales)
         wb_codes = keep.tile([P, 2 * N], U8, name="wb_codes", align_bytes=64)
         nc.sync.dma_start(wb_codes[:].bitcast(I32), wb_words[0].bitcast(I32))
         list6 = load_list(offs6, "list6")
         list7 = load_list(offs7, "list7")
 
-        w_dealt_plane = keep.tile([P, R], U8, name="w_dealt_plane", align_bytes=64)
-        w_codes = keep.tile([P, 2 * R], U8, name="w_codes", align_bytes=64)
+        w_first = keep.tile([P, 3 * P], U8, name="w_first", align_bytes=64)
         xg_scales = keep.tile([P, J], U8, name="xg_scales", align_bytes=64)
         xg_words = keep.tile([P, J], U32, name="xg_words", align_bytes=64)
         spread(w_plane, w_rows)
-        deal(w_dealt_plane[:], w_plane[:])
         spread(x_plane, x_rows)
-        deal(w_codes[:].bitcast(U16), w_raw[:].bitcast(U16))
+        deal(w_first[:, 0:P], w_plane[:], 0, 1)
+        deal(w_first[:, P : 3 * P].bitcast(U16), w_raw[:].bitcast(U16), 0, 1)
         nc.vector.tensor_copy(xg_scales[:], x_plane[:].indirect(slot_list[:]))
         for half in range(2):
             nc.vector.tensor_copy(
                 xg_words[:, J // 2 * half : J // 2 * (half + 1)],
                 x_words[:].indirect(slot_list[:, J // 32 * half : J // 32 * (half + 1)]),
             )
-
-        spread(w2_plane, w2_rows)
+        w_rest = keep.tile([P, 9 * P], U8, name="w_rest", tag="x_words", align_bytes=64)
+        deal(w_rest[:, 0 : 3 * P], w_plane[:], 1, PACK)
+        deal(w_rest[:, 3 * P : 9 * P].bitcast(U16), w_raw[:].bitcast(U16), 1, PACK)
+        w_operands = [(w_first[:, P : 3 * P], w_first[:, 0:P])] + [
+            (w_rest[:, (3 + 2 * u) * P : (5 + 2 * u) * P], w_rest[:, u * P : (u + 1) * P]) for u in range(PACK - 1)
+        ]
 
         banks = list(range(8))
 
@@ -135,14 +135,14 @@ def tile_list_gatedsum_twow_one_pagetwice_kernel(
                 banks.append(bank)
                 acc = psum.tile([P, J // pieces], F32, name=f"acc_{name}{t}_{piece}", tag=f"bank{bank}")
                 nc.tensor.matmul_mx(
-                    acc[:], lhsT=codes, lhsT_scale=plane[:, P * t : P * (t + 1)],
+                    acc[:], lhsT=codes, lhsT_scale=plane,
                     rhs=xg_words[:, cols].bitcast(E5M2X4), rhs_scale=xg_scales[:, cols], start=True, stop=True,
                 )
                 accs.append((cols, acc))
             return accs
 
         def looks(name, t, accs, val, gate, val_list, gate_list, weight, slope, offset):
-            rows = keep.tile([P, J], F32, name=f"{name}{t}")
+            rows = keep.tile([P, J], F32, name=f"{name}{t}", tag=f"{name}{t}")
             for cols, acc in accs:
                 nc.vector.tensor_copy(rows[:, cols], acc[:])
             col = slice(t, t + 1)
@@ -159,18 +159,23 @@ def tile_list_gatedsum_twow_one_pagetwice_kernel(
         w2_codes = keep.tile([P, R], U32, name="w2_codes", tag="w2_codes", align_bytes=64)
 
         a_acc = [
-            product("a", t, w_codes[:, 2 * P * t : 2 * P * (t + 1)].bitcast(E2M1X4), w_dealt_plane, 2 if t == 0 else 1)
+            product("a", t, w_operands[t][0].bitcast(E2M1X4), w_operands[t][1], 2 if t == 0 else 1)
             for t in range(PACK)
         ]
         for t in range(PACK):
             looks("a", t, a_acc[t], a_val, a_gate, list2, list3, sa_t, sg_t, bg_t)
-            if t == 0:
-                deal(w2_dealt_plane[:], w2_plane[:])
             if t == 1:
+                deal(w2_dealt_plane[:], w2_plane[:])
                 deal_words(w2_codes[:], w2_raw[:])
         for t in range(PACK):
-            acc = product("b", t, w2_codes[:, P * t : P * (t + 1)].bitcast(E4M3X4), w2_dealt_plane)
+            acc = product("b", t, w2_codes[:, P * t : P * (t + 1)].bitcast(E4M3X4), w2_dealt_plane[:, P * t : P * (t + 1)])
             looks("b", t, acc, b_val, b_gate, list4, list5, sb_t, sh_t, bh_t)
+
+        pages = {}
+        for (name, h), tag in zip((("pa", 0), ("pb", 0), ("pa", 1), ("pb", 1)), ("a2", "a3", "b0", "b1")):
+            page = keep.tile([P, E], F32, name=f"{name}{h}", tag=tag)
+            nc.gpsimd.memset(page[:], 0.0)
+            pages[name, h] = page
 
         a_term = keep.tile([P, PACK, O], F32, name="a_term", tag="w2_codes", align_bytes=64)
         b_term = keep.tile([P, PACK, O], F32, name="b_term")
@@ -180,7 +185,9 @@ def tile_list_gatedsum_twow_one_pagetwice_kernel(
         for lo, hi in ((0, 2), (2, 3), (3, 4)):
             nc.vector.tensor_tensor(b_term[:, lo:hi, :], b_val[:, lo:hi, :], b_gate[:, lo:hi, :], ALU.mult)
             nc.vector.tensor_tensor(summed[:, lo:hi, :], a_term[:, lo:hi, :], b_term[:, lo:hi, :], ALU.add)
-        nc.vector.tensor_scalar_max(hid[:], summed[:].rearrange("p t o -> p o t"), 0.0)
+            if hi == 2:
+                nc.vector.tensor_scalar_max(hid[:, :, 0:2], summed[:, 0:2, :].rearrange("p t o -> p o t"), 0.0)
+        nc.scalar.activation(hid[:, :, 2:4], summed[:, 2:4, :].rearrange("p t o -> p o t"), ACT.Relu)
         hid_codes = keep.tile([P, O], U32, name="hid_codes", align_bytes=64)
         hid_scales = keep.tile([P, O], U8, name="hid_scales", align_bytes=64)
         nc.vector.quantize_mx(hid_codes[:].bitcast(E4M3X4), hid_scales[:], hid[:].rearrange("p o t -> p (o t)"))
@@ -194,10 +201,7 @@ def tile_list_gatedsum_twow_one_pagetwice_kernel(
                 rhs=hid_codes[:].bitcast(E4M3X4), rhs_scale=hid_scales[:], start=True, stop=True,
             )
             rows = keep.tile([P, O], F32, name=f"p{h}")
-            if h == 0:
-                nc.vector.tensor_copy(rows[:], acc[:])
-            else:
-                nc.scalar.copy(rows[:], acc[:])
+            nc.scalar.copy(rows[:], acc[:])
             p_tiles.append(rows)
         for h in range(2):
             nc.vector.tensor_copy(pages["pa", h][:].indirect(list6[:]), p_tiles[h][:])

from contextlib import ExitStack

import concourse.mybir as mybir

K, T, J, R, O, N, E = 512, 1024, 256, 512, 128, 256, 512
FLOPS = 2 * (2 * K * R * J + R * N * O)

F32 = mybir.dt.float32
BF16 = mybir.dt.bfloat16
I32 = mybir.dt.int32
U32 = mybir.dt.uint32
U16 = mybir.dt.uint16
U8 = mybir.dt.uint8
E4M3X4 = mybir.dt.float8_e4m3fn_x4
E5M2X4 = mybir.dt.float8_e5m2_x4
E2M1X4 = mybir.dt.float4_e2m1fn_x4
ACT = mybir.ActivationFunctionType
ALU = mybir.AluOpType

P = 128
PACK = 4
QUADS = 4
QUAD = 32


def tile_list_gatedsum_twow_one_pagetwice_kernel(
    tc, xt_words, xt_scales, w_words, w_scales, w2_words, w2_scales, sa, sb, sg, bg, sh, bh,
    wb_words, wb_scales, offs, offs2, offs3, offs4, offs5, offs6, offs7, out,
):
    nc = tc.nc
    with ExitStack() as ctx:
        lists = ctx.enter_context(tc.tile_pool(name="lists", bufs=1))
        keep = ctx.enter_context(tc.tile_pool(name="keep", bufs=1))
        psum = ctx.enter_context(tc.psum_pool(name="psum", bufs=1))

        def load_list(src, name):
            tile = lists.tile(list(src.shape), U16, name=name)
            nc.sync.dma_start(tile[:], src)
            return tile

        def load_rows(src, name, queue=nc.sync):
            tile = keep.tile([P, PACK], F32, name=name)
            queue.dma_start(tile[:], src.rearrange("(p t) one -> p (t one)", t=PACK))
            return tile

        def load_scale_rows(src, name, queue=nc.sync):
            words = src.shape[2] // 4
            tile = keep.tile([4, QUADS, words], I32, name=name)
            queue.dma_start(tile[:], src[0].bitcast(I32).rearrange("(q r) c -> r q c", q=QUADS))
            return tile

        def zeroed_plane(width, name):
            plane = keep.tile([P, width], U8, name=name, align_bytes=64)
            nc.vector.memset(plane[:].bitcast(I32), 0)
            return plane

        def load_plane(plane, src):
            for q in range(QUADS):
                nc.sync.dma_start(
                    plane[QUAD * q : QUAD * q + 4, :].bitcast(I32), src[0, 4 * q : 4 * q + 4, :].bitcast(I32)
                )

        def spread(plane, staged):
            for q in range(QUADS):
                nc.vector.tensor_copy(plane[QUAD * q : QUAD * q + 4, :].bitcast(I32), staged[:, q, :])

        def deal(dst, src, lo=0, hi=PACK):
            nc.vector.tensor_copy(
                dst.rearrange("p (t m) -> p t m", m=P), src.rearrange("p (m t) -> p t m", t=PACK)[:, lo:hi, :]
            )

        def deal_words(dst, src):
            nc.vector.tensor_copy(
                dst.rearrange("p (t c i) -> p c t i", t=PACK, i=4), src.rearrange("p (c i t) -> p c t i", t=PACK, i=4)
            )

        x_plane = zeroed_plane(T, "x_plane")
        w_plane = zeroed_plane(R, "w_plane")
        w2_plane = zeroed_plane(R, "w2_plane")
        wb_plane = zeroed_plane(N, "wb_plane")

        w_rows = load_scale_rows(w_scales, "w_rows")
        sg_t = load_rows(sg, "sg_t", nc.scalar)
        x_rows = load_scale_rows(xt_scales, "x_rows")
        w_raw = keep.tile([P, 2 * R], U8, name="w_raw", align_bytes=64)
        nc.scalar.dma_start(w_raw[:].bitcast(I32), w_words[0].bitcast(I32))
        slot_list = load_list(offs, "slot_list")
        x_words = keep.tile([P, T], U32, name="x_words", tag="x_words", align_bytes=64)
        nc.scalar.dma_start(x_words[:].bitcast(I32), xt_words[0].rearrange("p c t -> p (c t)").bitcast(I32))
        list3 = load_list(offs3, "list3")
        bg_t = load_rows(bg, "bg_t")
        sh_t = load_rows(sh, "sh_t", nc.gpsimd)
        bh_t = load_rows(bh, "bh_t", nc.gpsimd)
        list2 = load_list(offs2, "list2")
        sa_t = load_rows(sa, "sa_t")
        list5 = load_list(offs5, "list5")
        list4 = load_list(offs4, "list4")
        sb_t = load_rows(sb, "sb_t")
        load_plane(w2_plane, w2_scales)
        w2_raw = keep.tile([P, R], U32, name="w2_raw", align_bytes=64)
        nc.sync.dma_start(w2_raw[:].bitcast(I32), w2_words[0].rearrange("p c t -> p (c t)").bitcast(I32))
        load_plane(wb_plane, wb_scales)
        wb_codes = keep.tile([P, 2 * N], U8, name="wb_codes", align_bytes=64)
        nc.sync.dma_start(wb_codes[:].bitcast(I32), wb_words[0].bitcast(I32))
        list6 = load_list(offs6, "list6")
        list7 = load_list(offs7, "list7")

        w_first = keep.tile([P, 3 * P], U8, name="w_first", align_bytes=64)
        xg_scales = keep.tile([P, J], U8, name="xg_scales", align_bytes=64)
        xg_words = keep.tile([P, J], U32, name="xg_words", align_bytes=64)
        spread(w_plane, w_rows)
        spread(x_plane, x_rows)
        deal(w_first[:, 0:P], w_plane[:], 0, 1)
        deal(w_first[:, P : 3 * P].bitcast(U16), w_raw[:].bitcast(U16), 0, 1)
        nc.vector.tensor_copy(xg_scales[:], x_plane[:].indirect(slot_list[:]))
        for half in range(2):
            nc.vector.tensor_copy(
                xg_words[:, J // 2 * half : J // 2 * (half + 1)],
                x_words[:].indirect(slot_list[:, J // 32 * half : J // 32 * (half + 1)]),
            )
        w_rest = keep.tile([P, 9 * P], U8, name="w_rest", tag="x_words", align_bytes=64)
        deal(w_rest[:, 0 : 3 * P], w_plane[:], 1, PACK)
        deal(w_rest[:, 3 * P : 9 * P].bitcast(U16), w_raw[:].bitcast(U16), 1, PACK)
        w_operands = [(w_first[:, P : 3 * P], w_first[:, 0:P])] + [
            (w_rest[:, (3 + 2 * u) * P : (5 + 2 * u) * P], w_rest[:, u * P : (u + 1) * P]) for u in range(PACK - 1)
        ]

        banks = list(range(8))

        def product(name, t, codes, plane, pieces=1):
            accs = []
            for piece in range(pieces):
                cols = slice(J // pieces * piece, J // pieces * (piece + 1))
                bank = banks.pop(0)
                banks.append(bank)
                acc = psum.tile([P, J // pieces], F32, name=f"acc_{name}{t}_{piece}", tag=f"bank{bank}")
                nc.tensor.matmul_mx(
                    acc[:], lhsT=codes, lhsT_scale=plane,
                    rhs=xg_words[:, cols].bitcast(E5M2X4), rhs_scale=xg_scales[:, cols], start=True, stop=True,
                )
                accs.append((cols, acc))
            return accs

        def looks(name, t, accs, val, gate, val_list, gate_list, weight, slope, offset):
            rows = keep.tile([P, J], F32, name=f"{name}{t}", tag=f"{name}{t}")
            for cols, acc in accs:
                nc.vector.tensor_copy(rows[:, cols], acc[:])
            col = slice(t, t + 1)
            nc.scalar.activation(
                gate[:, t, :], rows[:].indirect(gate_list[:]), ACT.Sigmoid, bias=offset[:, col], scale=slope[:, col]
            )
            nc.scalar.activation(val[:, t, :], rows[:].indirect(val_list[:]), ACT.Copy, scale=weight[:, col])

        a_val = keep.tile([P, PACK, O], F32, name="a_val")
        a_gate = keep.tile([P, PACK, O], F32, name="a_gate")
        b_val = keep.tile([P, PACK, O], F32, name="b_val")
        b_gate = keep.tile([P, PACK, O], F32, name="b_gate")
        w2_dealt_plane = keep.tile([P, R], U8, name="w2_dealt_plane", align_bytes=64)
        w2_codes = keep.tile([P, R], U32, name="w2_codes", tag="w2_codes", align_bytes=64)

        a_acc = [
            product("a", t, w_operands[t][0].bitcast(E2M1X4), w_operands[t][1], 2 if t == 0 else 1)
            for t in range(PACK)
        ]
        for t in range(PACK):
            looks("a", t, a_acc[t], a_val, a_gate, list2, list3, sa_t, sg_t, bg_t)
            if t == 1:
                deal(w2_dealt_plane[:], w2_plane[:])
                deal_words(w2_codes[:], w2_raw[:])
        for t in range(PACK):
            acc = product("b", t, w2_codes[:, P * t : P * (t + 1)].bitcast(E4M3X4), w2_dealt_plane[:, P * t : P * (t + 1)])
            looks("b", t, acc, b_val, b_gate, list4, list5, sb_t, sh_t, bh_t)

        pages = {}
        for (name, h), tag in zip((("pa", 0), ("pb", 0), ("pa", 1), ("pb", 1)), ("a2", "a3", "b0", "b1")):
            page = keep.tile([P, E], F32, name=f"{name}{h}", tag=tag)
            nc.gpsimd.memset(page[:], 0.0)
            pages[name, h] = page

        a_term = keep.tile([P, PACK, O], F32, name="a_term", tag="w2_codes", align_bytes=64)
        b_term = keep.tile([P, PACK, O], F32, name="b_term")
        summed = keep.tile([P, PACK, O], F32, name="summed")
        nc.vector.tensor_tensor(a_term[:], a_val[:], a_gate[:], ALU.mult)
        hid = keep.tile([P, O, PACK], BF16, name="hid", align_bytes=64)
        for lo, hi in ((0, 2), (2, 3), (3, 4)):
            nc.vector.tensor_tensor(b_term[:, lo:hi, :], b_val[:, lo:hi, :], b_gate[:, lo:hi, :], ALU.mult)
            nc.vector.tensor_tensor(summed[:, lo:hi, :], a_term[:, lo:hi, :], b_term[:, lo:hi, :], ALU.add)
            if hi == 2:
                nc.vector.tensor_scalar_max(hid[:, :, 0:2], summed[:, 0:2, :].rearrange("p t o -> p o t"), 0.0)
        nc.scalar.activation(hid[:, :, 2:4], summed[:, 2:4, :].rearrange("p t o -> p o t"), ACT.Relu)
        hid_codes = keep.tile([P, O], U32, name="hid_codes", align_bytes=64)
        hid_scales = keep.tile([P, O], U8, name="hid_scales", align_bytes=64)
        nc.vector.quantize_mx(hid_codes[:].bitcast(E4M3X4), hid_scales[:], hid[:].rearrange("p o t -> p (o t)"))

        p_tiles = []
        for h in range(2):
            acc = psum.tile([P, O], F32, name=f"acc_p{h}", tag=f"bank{1 + h}")
            nc.tensor.matmul_mx(
                acc[:], lhsT=wb_codes[:, 2 * P * h : 2 * P * (h + 1)].bitcast(E2M1X4),
                lhsT_scale=wb_plane[:, P * h : P * (h + 1)],
                rhs=hid_codes[:].bitcast(E4M3X4), rhs_scale=hid_scales[:], start=True, stop=True,
            )
            rows = keep.tile([P, O], F32, name=f"p{h}")
            nc.scalar.copy(rows[:], acc[:])
            p_tiles.append(rows)
        for h in range(2):
            nc.vector.tensor_copy(pages["pa", h][:].indirect(list6[:]), p_tiles[h][:])
            nc.scalar.activation(pages["pb", h][:].indirect(list7[:]), p_tiles[h][:], ACT.Copy)
            pieces = 2
            for piece in range(pieces):
                cols = slice(E // pieces * piece, E // pieces * (piece + 1))
                total = keep.tile([P, E // pieces], F32, name=f"total{h}{piece}")
                nc.vector.tensor_tensor(total[:], pages["pa", h][:, cols], pages["pb", h][:, cols], ALU.add)
                nc.sync.dma_start(out[P * h : P * (h + 1), cols], total[:])
